import numpy as np
import ml_dtypes


def mxq(x, axis, fmt="e4m3"):
    dtype, down = {"e4m3": (ml_dtypes.float8_e4m3fn, 7), "e5m2": (ml_dtypes.float8_e5m2, 14)}[fmt]
    v = np.moveaxis(np.asarray(x, np.float32).astype(ml_dtypes.bfloat16).astype(np.float64), axis, -1)
    blocks = v.reshape(v.shape[:-1] + (-1, 32))
    amax = np.abs(blocks).max(-1, keepdims=True)
    byte = np.maximum(np.where(amax > 0, np.frexp(amax)[1] - 1 + 127, 0) - down, 1)
    scale = np.exp2(byte - 127.0)
    codes = (blocks / scale).astype(np.float32).astype(dtype).astype(np.float64)
    return np.moveaxis((codes * scale).reshape(v.shape), -1, axis)


WIDE = False


def mx_kscale(k):
    if not WIDE:
        return np.ones(k)
    levels = np.array([10, -10, 5, -5, 0])
    if k % 512:
        return np.exp2(np.random.permutation(np.resize(levels, k // 32))).repeat(32)
    a = np.empty((k // 512, 16))
    for p in range(k // 512):
        a[p, :8] = np.random.permutation(np.resize(levels, 8))
        for g in range(8):
            far = levels[np.abs(levels - a[p, g]) >= 10]
            a[p, g + 8] = far[np.random.randint(len(far))]
    return np.exp2(a.ravel()).repeat(32)


def f64(x):
    return np.asarray(x).astype(np.float64)


def striped(idx):
    return np.tile(idx.reshape(-1, 16).T, (8, 1)).astype(np.uint16)


def unstriped(offs):
    return offs[:16].T.reshape(-1).astype(np.int64)


E2M1 = np.array([0.0, 0.5, 1.0, 1.5, 2.0, 3.0, 4.0, 6.0, -0.0, -0.5, -1.0, -1.5, -2.0, -3.0, -4.0, -6.0])


def pack_weight(w, fmt):
    k, n = w.shape
    w = f64(np.asarray(w, np.float32).astype(ml_dtypes.bfloat16)).reshape(k // 32, 32, n)
    amax = np.abs(w).max(1)
    if fmt == "e4m3":
        byte = np.frexp(amax)[1] - 1 + 127 - 7
    else:
        mant, ex = np.frexp(amax / 6.0)
        byte = np.where(mant > 0.5, ex, ex - 1) + 127
    byte = np.clip(np.where(amax > 0, byte, 1), 1, 254)
    scaled = (w * np.exp2(127.0 - byte)[:, None, :]).reshape(k, n).astype(np.float32)
    by_word = np.ascontiguousarray(scaled.reshape(k // 512, 128, 4, n).transpose(0, 1, 3, 2))
    if fmt == "e4m3":
        words = by_word.astype(ml_dtypes.float8_e4m3fn).view(np.uint8)
    else:
        c = by_word.astype(ml_dtypes.float4_e2m1fn).view(np.uint8) & 0xF
        words = (c[..., 0::2] | (c[..., 1::2] << 4)).reshape(k // 512, 128, 2 * n)
    return np.ascontiguousarray(words), np.ascontiguousarray(byte.astype(np.uint8).reshape(k // 512, 16, n))


def unpack_weight(words, scales, fmt):
    g, _, n = scales.shape
    words = np.ascontiguousarray(words).reshape(g, 128, n, -1)
    if fmt == "e4m3":
        vals = words.view(ml_dtypes.float8_e4m3fn).astype(np.float64)
    else:
        nib = np.empty((g, 128, n, 4), np.uint8)
        nib[..., 0::2] = words & 0xF
        nib[..., 1::2] = words >> 4
        vals = E2M1[nib]
    vals = vals * np.repeat(np.exp2(scales.astype(np.float64) - 127.0), 8, axis=1)[..., None]
    return vals.transpose(0, 1, 3, 2).reshape(g * 512, n)


def gelu(v):
    return 0.5 * v * (1.0 + np.tanh(np.sqrt(2.0 / np.pi) * (v + 0.044715 * v**3)))


def striped8(idx):
    return np.concatenate([v.reshape(-1, 16).T for v in idx]).astype(np.uint16)


def unstriped8(offs):
    return np.stack([offs[16 * g:16 * g + 16].T.reshape(-1) for g in range(8)]).astype(np.int64)


def heads(h, wgt, idx8):
    r = np.arange(h.shape[0])
    return wgt[r // 4 % 128] * h[r[:, None], idx8[r % 512 // 64]]


K, H, N, T, S, T2, P = 1024, 512, 768, 4096, 1024, 2048, 1024

def setup_inputs():
    n = np.random.standard_normal
    s = mx_kscale(K)[:, None]
    u = mx_kscale(H)[:, None]
    tab_words, tab_scales = pack_weight(n((K, T)) * s, "e4m3")
    w2_words, w2_scales = pack_weight(0.55 * n((K, H)) / np.sqrt(K) / s, "e4m3")
    w4_words, w4_scales = pack_weight(n((H, N)) / np.sqrt(H) / u, "e2m1")
    return {
        "tab_words": tab_words, "tab_scales": tab_scales,
        "offs": striped(np.random.permutation(T)[:S]),
        "offs2": striped(np.random.permutation(T2)[:S]),
        "offs3": striped8(np.stack([np.random.permutation(T2)[:P] for _ in range(8)])),
        "w1": (1.2 * n((K, H)) / np.sqrt(K) / s).astype(np.float32),
        "w2_words": w2_words, "w2_scales": w2_scales,
        "rg": (np.exp(0.4 * n((H, S))) * u).astype(np.float32),
        "gain": (1.3 * np.exp(0.3 * n(H)) * u[:, 0]).astype(np.float32),
        "wgs": np.exp(0.3 * n((128, S))).astype(np.float32),
        "page0": (n((H, T2)) * u).astype(np.float32),
        "wgt": np.repeat(np.random.uniform(0.5, 2.0, (8, P)), 16, axis=0).astype(np.float32),
        "w3": (n((H, N)) / np.sqrt(H) / u).astype(np.float32),
        "w4_words": w4_words, "w4_scales": w4_scales,
    }

def reference(tab_words, tab_scales, offs, offs2, offs3, w1, w2_words, w2_scales, rg, gain, wgs, page0, wgt, w3, w4_words, w4_scales):
    v = unpack_weight(tab_words, tab_scales, "e4m3")[:, unstriped(offs)]
    w2 = unpack_weight(w2_words, w2_scales, "e4m3")
    a = mxq(f64(w1), 0, "e4m3").T @ v
    b = w2.T @ v
    h = np.tanh(a) * f64(rg) + np.sin(b) * f64(gain)[:, None]
    page = f64(page0).copy()
    page[:, unstriped(offs2)] = np.tile(f64(wgs), (H // 128, 1)) * h
    x = heads(page, f64(wgt), unstriped8(offs3))
    x = mxq(x, 0, "e4m3")
    w4 = unpack_weight(w4_words, w4_scales, "e2m1")
    y1 = mxq(f64(w3), 0, "e4m3").T @ x
    y2 = w4.T @ x
    return np.minimum(y1, y2)

@@ -1,0 +1,266 @@
+import math
+from contextlib import ExitStack
+
+import concourse.mybir as mybir
+
+K, H, N, T, S, T2, M = 1024, 512, 768, 4096, 1024, 2048, 1024
+FLOPS = 2 * (2 * K * H * S + 2 * H * N * M)
+
+F32 = mybir.dt.float32
+BF16 = mybir.dt.bfloat16
+I32 = mybir.dt.int32
+U32 = mybir.dt.uint32
+U16 = mybir.dt.uint16
+U8 = mybir.dt.uint8
+FP8X4 = mybir.dt.float8_e4m3fn_x4
+FP4X4 = mybir.dt.float4_e2m1fn_x4
+ALU = mybir.AluOpType
+ACT = mybir.ActivationFunctionType
+
+P = 128
+PACK = 4
+PASSES = K // (P * PACK)
+HALF = 512
+CHUNK = 256
+W3_HALF = N // 2
+ROUNDER = 1.5 * 2.0**23
+TWO_PI = 2.0 * math.pi
+
+
+def tile_list_encounter_cell_watch_kernel(
+    tc, tab_words, tab_scales, offs, offs2, offs3, w1, w2_words, w2_scales, rg, gain, wgs, page0, wgt, w3, w4_words, w4_scales, out
+):
+    nc = tc.nc
+    with ExitStack() as ctx:
+        keep = ctx.enter_context(tc.tile_pool(name="keep", bufs=1))
+        ring = ctx.enter_context(tc.tile_pool(name="ring", bufs=2))
+        psum = ctx.enter_context(tc.psum_pool(name="psum", bufs=4))
+
+        list1 = keep.tile([P, S // 16], U16, name="list1")
+        list2 = keep.tile([P, S // 16], U16, name="list2")
+        list3 = keep.tile([P, M // 16], U16, name="list3")
+
+        tab_sc = keep.tile([P, T], U8, name="tab_sc", align_bytes=64)
+        w2_sc_raw = keep.tile([P, H], U8, name="w2_sc_raw", align_bytes=64)
+        w4_sc = keep.tile([P, N], U8, name="w4_sc", align_bytes=64)
+        for plane in (tab_sc, w2_sc_raw, w4_sc):
+            nc.vector.memset(plane[:].bitcast(I32), 0)
+        gain_sb = keep.tile([P, PACK], F32, name="gain_sb")
+
+        nc.sync.dma_start(list1[:], offs)
+        tab = [keep.tile([P, T], I32, name=f"tab{a}", align_bytes=64) for a in range(PASSES)]
+        w2_raw = keep.tile([P, PASSES, H], I32, name="w2_raw", align_bytes=64)
+        nc.sync.dma_start(out=tab[0][:], in_=tab_words[0].rearrange("p t i -> p (t i)").bitcast(I32))
+        for q in range(4):
+            nc.sync.dma_start(out=tab_sc[32 * q : 32 * q + 8, :].bitcast(I32), in_=tab_scales[:, 4 * q : 4 * q + 4, :].bitcast(I32))
+        nc.sync.dma_start(out=w2_raw[:], in_=w2_words.rearrange("a p c i -> p a (c i)").bitcast(I32))
+        nc.sync.dma_start(out=tab[1][:], in_=tab_words[1].rearrange("p t i -> p (t i)").bitcast(I32))
+        for q in range(4):
+            nc.sync.dma_start(out=w2_sc_raw[32 * q : 32 * q + 8, :].bitcast(I32), in_=w2_scales[:, 4 * q : 4 * q + 4, :].bitcast(I32))
+        w1_raw = []
+        for a in range(PASSES):
+            raw = ring.tile([P, PACK, H], F32, name=f"w1_raw{a}", tag="w_raw")
+            nc.sync.dma_start(out=raw[:], in_=w1[512 * a : 512 * (a + 1), :].rearrange("(p j) c -> p j c", j=PACK))
+            w1_raw.append(raw)
+
+        nc.sync.dma_start(list2[:], offs2)
+        nc.sync.dma_start(out=gain_sb[:], in_=gain.rearrange("(p i) -> p i", i=PACK))
+        rg_rows = rg.rearrange("(p i) j -> p i j", i=PACK)
+        page_rows = page0.rearrange("(p i) t -> p i t", i=PACK)
+        wgs_rows = wgs.rearrange("(p i) j -> p i j", i=PACK)
+        rg_sb, page, wgs_sb = [], [], []
+        for i in range(PACK):
+            rg_sb.append(keep.tile([P, S], F32, name=f"rg{i}", tag=f"rg{i}"))
+            page.append(keep.tile([P, T2], F32, name=f"page{i}"))
+            wgs_sb.append(keep.tile([P, S], F32, name=f"wgs{i}", tag=f"wgs{i}"))
+            nc.sync.dma_start(out=rg_sb[i][:], in_=rg_rows[:, i, :])
+            nc.sync.dma_start(out=page[i][:], in_=page_rows[:, i, :])
+            for q in (0, 2, 1, 3):
+                nc.sync.dma_start(out=wgs_sb[i][32 * q : 32 * (q + 1), :], in_=wgs_rows[:, i, :])
+
+        nc.sync.dma_start(list3[:], offs3)
+        wgt_sb = keep.tile([P, M], F32, name="wgt_sb")
+        nc.sync.dma_start(out=wgt_sb[:], in_=wgt)
+        w4_codes = keep.tile([P, 2 * N], U8, name="w4_codes", align_bytes=64)
+        nc.sync.dma_start(out=w4_codes[:].bitcast(I32), in_=w4_words[0].bitcast(I32))
+
+        for q in range(4):
+            nc.sync.dma_start(out=w4_sc[32 * q : 32 * q + 4, :].bitcast(I32), in_=w4_scales[0, 4 * q : 4 * q + 4, :].bitcast(I32))
+        v_codes = [keep.tile([P, S], U32, name=f"v_codes{a}", align_bytes=64) for a in range(PASSES)]
+        v_sc = keep.tile([P, S], U8, name="v_sc", align_bytes=64)
+
+        def gather_words(a):
+            for hf in range(S // HALF):
+                nc.vector.tensor_copy(
+                    v_codes[a][:, hf * HALF : (hf + 1) * HALF],
+                    tab[a][:].bitcast(U32).indirect(list1[:, hf * HALF // 16 : (hf + 1) * HALF // 16]),
+                )
+
+        nc.vector.tensor_copy(v_sc[:], tab_sc[:].indirect(list1[:]))
+        gather_words(0)
+        w2_codes = keep.tile([P, PASSES, H], U32, name="w2_codes", align_bytes=64)
+        w2_sc = keep.tile([P, H], U8, name="w2_sc", align_bytes=64)
+        for a in range(PASSES):
+            nc.vector.tensor_copy(
+                w2_codes[:, a, :].rearrange("p (i m) -> p m i", i=PACK),
+                w2_raw[:, a, :].bitcast(U32).rearrange("p (m i) -> p m i", i=PACK),
+            )
+        nc.vector.tensor_copy(w2_sc[:].rearrange("p (i m) -> p m i", i=PACK), w2_sc_raw[:].rearrange("p (m i) -> p m i", i=PACK))
+        gather_words(1)
+
+        w1_codes, w1_sc = [], []
+        for a in range(PASSES):
+            grouped = ring.tile([P, H * PACK], BF16, name=f"w1_bf{a}", tag="w_bf", align_bytes=64)
+            nc.vector.tensor_copy(
+                grouped[:].rearrange("p (i m j) -> p m i j", i=PACK, j=PACK),
+                w1_raw[a][:].rearrange("p j (m i) -> p m i j", i=PACK),
+            )
+            w1_codes.append(keep.tile([P, H], U32, name=f"w1_codes{a}", align_bytes=64))
+            w1_sc.append(keep.tile([P, H], U8, name=f"w1_sc{a}", align_bytes=64))
+            nc.vector.quantize_mx(out=w1_codes[a][:].bitcast(FP8X4), scales=w1_sc[a][:], in_=grouped[:])
+
+        def first_product(acc, codes, scales, unit):
+            i, hf = divmod(unit, 2)
+            rows = slice(P * i, P * (i + 1))
+            cols = slice(hf * HALF, (hf + 1) * HALF)
+            for a in range(PASSES):
+                nc.tensor.matmul_mx(
+                    out=acc[:],
+                    lhsT=codes(a)[:, rows].bitcast(FP8X4),
+                    lhsT_scale=scales(a)[:, rows],
+                    rhs=v_codes[a][:, cols].bitcast(FP8X4),
+                    rhs_scale=v_sc[4 * a : P, cols],
+                    start=(a == 0),
+                    stop=(a == PASSES - 1),
+                )
+
+        sines, tanhs, hs = {}, {}, {}
+
+        def sine_part(unit):
+            b = psum.tile([P, HALF], F32, name="b", tag="bank_b")
+            first_product(b, lambda a: w2_codes[:, a, :], lambda a: w2_sc[4 * a : P, :], unit)
+            turns_biased = ring.tile([P, HALF], U32, name="turns_biased")
+            nc.scalar.activation(turns_biased[:], b[:], ACT.Copy, bias=ROUNDER, scale=1.0 / TWO_PI)
+            turns = ring.tile([P, HALF], F32, name="turns")
+            nc.scalar.activation(turns[:], turns_biased[:], ACT.Copy, bias=-ROUNDER, scale=1.0)
+            angle = ring.tile([P, HALF], F32, name="angle")
+            nc.vector.scalar_tensor_tensor(angle[:], turns[:], -TWO_PI, b[:], ALU.mult, ALU.add)
+            sines[unit] = ring.tile([P, HALF], F32, name="sine", bufs=4)
+            nc.scalar.activation(sines[unit][:], angle[:], ACT.Sin)
+
+        def tanh_part(unit):
+            acc = psum.tile([P, HALF], F32, name="acc", tag="bank_a")
+            first_product(acc, lambda a: w1_codes[a][:], lambda a: w1_sc[a][:], unit)
+            tanhs[unit] = ring.tile([P, HALF], F32, name="tanh", bufs=4)
+            nc.scalar.activation(tanhs[unit][:], acc[:], ACT.Tanh)
+
+        def ranged(unit):
+            i, hf = divmod(unit, 2)
+            tr = ring.tile([P, HALF], F32, name="tr")
+            nc.vector.tensor_tensor(tr[:], tanhs[unit][:], rg_sb[i][:, hf * HALF : (hf + 1) * HALF], ALU.mult)
+            return tr
+
+        def combine(unit, tr):
+            i = unit // 2
+            hs[unit] = ring.tile([P, HALF], F32, name="h")
+            nc.vector.scalar_tensor_tensor(hs[unit][:], sines[unit][:], gain_sb[:, i : i + 1], tr[:], ALU.mult, ALU.add)
+
+        def scatter(unit):
+            i, hf = divmod(unit, 2)
+            nc.vector.tensor_tensor(
+                page[i][:].indirect(list2[:, hf * HALF // 16 : (hf + 1) * HALF // 16]),
+                hs[unit][:],
+                wgs_sb[i][:, hf * HALF : (hf + 1) * HALF],
+                ALU.mult,
+            )
+
+        w3_codes, w3_sc = [], []
+
+        def quantise_w3(g):
+            raw = ring.tile([P, PACK, W3_HALF], F32, name=f"w3_raw{g}", tag="w_raw")
+            nc.sync.dma_start(out=raw[:], in_=w3.rearrange("(p j) n -> p j n", j=PACK)[:, :, g * W3_HALF : (g + 1) * W3_HALF])
+            grouped = ring.tile([P, W3_HALF * PACK], BF16, name=f"w3_bf{g}", tag="w_bf", align_bytes=64)
+            nc.scalar.copy(
+                grouped[:].rearrange("p (c e j) -> p c j e", e=4, j=PACK),
+                raw[:].rearrange("p j (c e) -> p c j e", e=4),
+            )
+            w3_codes.append(keep.tile([P, W3_HALF], U32, name=f"w3_codes{g}", align_bytes=64))
+            w3_sc.append(keep.tile([P, W3_HALF], U8, name=f"w3_sc{g}", align_bytes=64))
+            nc.vector.quantize_mx(out=w3_codes[g][:].bitcast(FP8X4), scales=w3_sc[g][:], in_=grouped[:])
+
+        sine_part(0)
+        sine_part(1)
+        for i in range(PACK):
+            units = (2 * i, 2 * i + 1)
+            for u in units:
+                tanh_part(u)
+            trs = [ranged(u) for u in units]
+            for u, tr in zip(units, trs):
+                combine(u, tr)
+            for u in units:
+                if u + 2 < 2 * PACK:
+                    sine_part(u + 2)
+                scatter(u)
+        for g in range(2):
+            quantise_w3(g)
+
+        x_codes, x_sc = {}, {}
+
+        def gather_x(c):
+            cols = slice(c * CHUNK, (c + 1) * CHUNK)
+            xg = keep.tile([P, PACK, CHUNK], F32, name=f"xg{c}", tag=("wgs3", "rg3")[c % 2])
+            for i in range(PACK):
+                nc.vector.tensor_tensor(
+                    xg[:, i, :], page[i][:].indirect(list3[:, c * CHUNK // 16 : (c + 1) * CHUNK // 16]), wgt_sb[:, cols], ALU.mult
+                )
+            xb = ring.tile([P, CHUNK * PACK], BF16, name="xb", align_bytes=64)
+            nc.scalar.copy(xb[:].rearrange("p (c e i) -> p c i e", e=4, i=PACK), xg[:].rearrange("p i (c e) -> p c i e", e=4))
+            return xb
+
+        def quantise_x(c, xb):
+            x_codes[c] = ring.tile([P, CHUNK], U32, name="x_codes", align_bytes=64)
+            x_sc[c] = ring.tile([P, CHUNK], U8, name="x_sc", align_bytes=64)
+            nc.vector.quantize_mx(out=x_codes[c][:].bitcast(FP8X4), scales=x_sc[c][:], in_=xb[:])
+
+        def second_products(c):
+            for pair in range(N // (2 * P)):
+                y1 = psum.tile([P, 2, CHUNK], F32, name="y1", tag="bank_a")
+                y2 = psum.tile([P, 2, CHUNK], F32, name="y2", tag="bank_b")
+                for e in range(2):
+                    n0 = (2 * pair + e) * P
+                    nc.tensor.matmul_mx(
+                        out=y2[:, e, :],
+                        lhsT=w4_codes[:, 2 * n0 : 2 * (n0 + P)].bitcast(FP4X4),
+                        lhsT_scale=w4_sc[:, n0 : n0 + P],
+                        rhs=x_codes[c][:].bitcast(FP8X4),
+                        rhs_scale=x_sc[c][:],
+                        start=True,
+                        stop=True,
+                    )
+                for e in range(2):
+                    g, n0 = divmod((2 * pair + e) * P, W3_HALF)
+                    nc.tensor.matmul_mx(
+                        out=y1[:, e, :],
+                        lhsT=w3_codes[g][:, n0 : n0 + P].bitcast(FP8X4),
+                        lhsT_scale=w3_sc[g][:, n0 : n0 + P],
+                        rhs=x_codes[c][:].bitcast(FP8X4),
+                        rhs_scale=x_sc[c][:],
+                        start=True,
+                        stop=True,
+                    )
+                y2_sb = ring.tile([P, 2, CHUNK], F32, name="y2_sb")
+                nc.scalar.copy(y2_sb[:], y2[:])
+                low = ring.tile([P, 2, CHUNK], F32, name="low", bufs=4)
+                nc.vector.tensor_tensor(low[:], y1[:], y2_sb[:], ALU.min)
+                rows = out[2 * pair * P : 2 * (pair + 1) * P, c * CHUNK : (c + 1) * CHUNK]
+                nc.sync.dma_start(out=rows.rearrange("(e p) m -> p e m", p=P), in_=low[:])
+
+        chunks = M // CHUNK
+        xbs = {0: gather_x(0)}
+        for c in range(chunks):
+            if c + 1 < chunks:
+                xbs[c + 1] = gather_x(c + 1)
+            quantise_x(c, xbs[c])
+            if c >= 1:
+                second_products(c - 1)
+        second_products(chunks - 1)

@@ -40,28 +40,30 @@ def tile_list_encounter_cell_watch_kernel(
         list2 = keep.tile([P, S // 16], U16, name="list2")
         list3 = keep.tile([P, M // 16], U16, name="list3")
 
-        tab_sc = keep.tile([P, T], U8, name="tab_sc", align_bytes=64)
-        w2_sc_raw = keep.tile([P, H], U8, name="w2_sc_raw", align_bytes=64)
+        tab_sc = keep.tile([P, T], U8, name="tab_sc", tag="v_codes1", align_bytes=64)
+        w2_sc_raw = keep.tile([P, H], U8, name="w2_sc_raw", tag="w1_bf0", align_bytes=64)
         w4_sc = keep.tile([P, N], U8, name="w4_sc", align_bytes=64)
         for plane in (tab_sc, w2_sc_raw, w4_sc):
             nc.vector.memset(plane[:].bitcast(I32), 0)
+        for q in range(4):
+            nc.gpsimd.dma_start(out=tab_sc[32 * q : 32 * q + 8, :].bitcast(I32), in_=tab_scales[:, 4 * q : 4 * q + 4, :].bitcast(I32))
+        for q in range(4):
+            nc.gpsimd.dma_start(out=w2_sc_raw[32 * q : 32 * q + 8, :].bitcast(I32), in_=w2_scales[:, 4 * q : 4 * q + 4, :].bitcast(I32))
         gain_sb = keep.tile([P, PACK], F32, name="gain_sb")
 
         nc.sync.dma_start(list1[:], offs)
         tab = [keep.tile([P, T], I32, name=f"tab{a}", align_bytes=64) for a in range(PASSES)]
         w2_raw = keep.tile([P, PASSES, H], I32, name="w2_raw", align_bytes=64)
         nc.sync.dma_start(out=tab[0][:], in_=tab_words[0].rearrange("p t i -> p (t i)").bitcast(I32))
-        for q in range(4):
-            nc.sync.dma_start(out=tab_sc[32 * q : 32 * q + 8, :].bitcast(I32), in_=tab_scales[:, 4 * q : 4 * q + 4, :].bitcast(I32))
         nc.sync.dma_start(out=w2_raw[:], in_=w2_words.rearrange("a p c i -> p a (c i)").bitcast(I32))
         nc.sync.dma_start(out=tab[1][:], in_=tab_words[1].rearrange("p t i -> p (t i)").bitcast(I32))
-        for q in range(4):
-            nc.sync.dma_start(out=w2_sc_raw[32 * q : 32 * q + 8, :].bitcast(I32), in_=w2_scales[:, 4 * q : 4 * q + 4, :].bitcast(I32))
         w1_raw = []
         for a in range(PASSES):
-            raw = ring.tile([P, PACK, H], F32, name=f"w1_raw{a}", tag="w_raw")
-            nc.sync.dma_start(out=raw[:], in_=w1[512 * a : 512 * (a + 1), :].rearrange("(p j) c -> p j c", j=PACK))
-            w1_raw.append(raw)
+            rows = w1[512 * a : 512 * (a + 1), :].rearrange("(p j) c -> p j c", j=PACK)
+            for g in range(2):
+                raw = ring.tile([P, PACK, H // 2], F32, name=f"w1_raw{a}{g}", tag="w_raw", bufs=4)
+                nc.sync.dma_start(out=raw[:], in_=rows[:, :, g * H // 2 : (g + 1) * H // 2])
+                w1_raw.append(raw)
 
         nc.sync.dma_start(list2[:], offs2)
         nc.sync.dma_start(out=gain_sb[:], in_=gain.rearrange("(p i) -> p i", i=PACK))
@@ -73,10 +75,13 @@ def tile_list_encounter_cell_watch_kernel(
             rg_sb.append(keep.tile([P, S], F32, name=f"rg{i}", tag=f"rg{i}"))
             page.append(keep.tile([P, T2], F32, name=f"page{i}"))
             wgs_sb.append(keep.tile([P, S], F32, name=f"wgs{i}", tag=f"wgs{i}"))
-            nc.sync.dma_start(out=rg_sb[i][:], in_=rg_rows[:, i, :])
-            nc.sync.dma_start(out=page[i][:], in_=page_rows[:, i, :])
-            for q in (0, 2, 1, 3):
-                nc.sync.dma_start(out=wgs_sb[i][32 * q : 32 * (q + 1), :], in_=wgs_rows[:, i, :])
+            for hf in range(S // HALF):
+                cols = slice(hf * HALF, (hf + 1) * HALF)
+                nc.sync.dma_start(out=rg_sb[i][:, cols], in_=rg_rows[:, i, cols])
+                if hf == 0:
+                    nc.sync.dma_start(out=page[i][:], in_=page_rows[:, i, :])
+                for q in (0, 2, 1, 3):
+                    nc.sync.dma_start(out=wgs_sb[i][32 * q : 32 * (q + 1), cols], in_=wgs_rows[:, i, cols])
 
         nc.sync.dma_start(list3[:], offs3)
         wgt_sb = keep.tile([P, M], F32, name="wgt_sb")
@@ -84,9 +89,13 @@ def tile_list_encounter_cell_watch_kernel(
         w4_codes = keep.tile([P, 2 * N], U8, name="w4_codes", align_bytes=64)
         nc.sync.dma_start(out=w4_codes[:].bitcast(I32), in_=w4_words[0].bitcast(I32))
 
+        zero = keep.tile([P, 1], F32, name="zero")
+        nc.vector.memset(zero[:], 0.0)
+        warm = keep.tile([P, 1], F32, name="warm")
+        nc.scalar.activation(warm[:], zero[:], ACT.Silu)
         for q in range(4):
             nc.sync.dma_start(out=w4_sc[32 * q : 32 * q + 4, :].bitcast(I32), in_=w4_scales[0, 4 * q : 4 * q + 4, :].bitcast(I32))
-        v_codes = [keep.tile([P, S], U32, name=f"v_codes{a}", align_bytes=64) for a in range(PASSES)]
+        v_codes = [keep.tile([P, S], U32, name=f"v_codes{a}", tag=f"v_codes{a}", align_bytes=64) for a in range(PASSES)]
         v_sc = keep.tile([P, S], U8, name="v_sc", align_bytes=64)
 
         def gather_words(a):
@@ -110,14 +119,19 @@ def tile_list_encounter_cell_watch_kernel(
 
         w1_codes, w1_sc = [], []
         for a in range(PASSES):
-            grouped = ring.tile([P, H * PACK], BF16, name=f"w1_bf{a}", tag="w_bf", align_bytes=64)
-            nc.vector.tensor_copy(
-                grouped[:].rearrange("p (i m j) -> p m i j", i=PACK, j=PACK),
-                w1_raw[a][:].rearrange("p j (m i) -> p m i j", i=PACK),
-            )
+            grouped = keep.tile([P, H * PACK], BF16, name=f"w1_bf{a}", tag=f"w1_bf{a}", align_bytes=64)
+            for g in range(2):
+                nc.vector.tensor_copy(
+                    grouped[:].rearrange("p (i m j) -> p m i j", i=PACK, j=PACK)[:, g * P // 2 : (g + 1) * P // 2],
+                    w1_raw[2 * a + g][:].rearrange("p j (m i) -> p m i j", i=PACK),
+                )
             w1_codes.append(keep.tile([P, H], U32, name=f"w1_codes{a}", align_bytes=64))
             w1_sc.append(keep.tile([P, H], U8, name=f"w1_sc{a}", align_bytes=64))
-            nc.vector.quantize_mx(out=w1_codes[a][:].bitcast(FP8X4), scales=w1_sc[a][:], in_=grouped[:])
+            for g in range(2):
+                cols = slice(g * H // 2, (g + 1) * H // 2)
+                nc.vector.quantize_mx(
+                    out=w1_codes[a][:, cols].bitcast(FP8X4), scales=w1_sc[a][:, cols], in_=grouped[:, g * 2 * H : (g + 1) * 2 * H]
+                )
 
         def first_product(acc, codes, scales, unit):
             i, hf = divmod(unit, 2)
@@ -177,9 +191,9 @@ def tile_list_encounter_cell_watch_kernel(
         w3_codes, w3_sc = [], []
 
         def quantise_w3(g):
-            raw = ring.tile([P, PACK, W3_HALF], F32, name=f"w3_raw{g}", tag="w_raw")
+            raw = ring.tile([P, PACK, W3_HALF], F32, name=f"w3_raw{g}", tag="w_raw", bufs=4)
             nc.sync.dma_start(out=raw[:], in_=w3.rearrange("(p j) n -> p j n", j=PACK)[:, :, g * W3_HALF : (g + 1) * W3_HALF])
-            grouped = ring.tile([P, W3_HALF * PACK], BF16, name=f"w3_bf{g}", tag="w_bf", align_bytes=64)
+            grouped = keep.tile([P, W3_HALF * PACK], BF16, name=f"w3_bf{g}", tag=f"w1_bf{g}", align_bytes=64)
             nc.scalar.copy(
                 grouped[:].rearrange("p (c e j) -> p c j e", e=4, j=PACK),
                 raw[:].rearrange("p j (c e) -> p c j e", e=4),

@@ -2,6 +2,7 @@ import math
 from contextlib import ExitStack
 
 import concourse.mybir as mybir
+from concourse.masks import make_identity
 
 K, H, N, T, S, T2, M = 1024, 512, 768, 4096, 1024, 2048, 1024
 FLOPS = 2 * (2 * K * H * S + 2 * H * N * M)
@@ -27,6 +28,10 @@ ROUNDER = 1.5 * 2.0**23
 TWO_PI = 2.0 * math.pi
 
 
+def pieces(i):
+    return [slice(0, HALF), slice(HALF, S)] if i == 0 else [slice(0, S)]
+
+
 def tile_list_encounter_cell_watch_kernel(
     tc, tab_words, tab_scales, offs, offs2, offs3, w1, w2_words, w2_scales, rg, gain, wgs, page0, wgt, w3, w4_words, w4_scales, out
 ):
@@ -34,37 +39,36 @@ def tile_list_encounter_cell_watch_kernel(
     with ExitStack() as ctx:
         keep = ctx.enter_context(tc.tile_pool(name="keep", bufs=1))
         ring = ctx.enter_context(tc.tile_pool(name="ring", bufs=2))
-        psum = ctx.enter_context(tc.psum_pool(name="psum", bufs=4))
+        psum = ctx.enter_context(tc.psum_pool(name="psum", bufs=1))
+        banks = [psum.tile([P, HALF], F32, name=f"bank{n}") for n in range(8)]
 
         list1 = keep.tile([P, S // 16], U16, name="list1")
         list2 = keep.tile([P, S // 16], U16, name="list2")
         list3 = keep.tile([P, M // 16], U16, name="list3")
 
         tab_sc = keep.tile([P, T], U8, name="tab_sc", tag="v_codes1", align_bytes=64)
-        w2_sc_raw = keep.tile([P, H], U8, name="w2_sc_raw", tag="w1_bf0", align_bytes=64)
+        w2_sc_raw = keep.tile([P, H], U8, name="w2_sc_raw", align_bytes=64)
         w4_sc = keep.tile([P, N], U8, name="w4_sc", align_bytes=64)
-        for plane in (tab_sc, w2_sc_raw, w4_sc):
+        for plane in (w2_sc_raw, tab_sc, w4_sc):
             nc.vector.memset(plane[:].bitcast(I32), 0)
         for q in range(4):
             nc.gpsimd.dma_start(out=tab_sc[32 * q : 32 * q + 8, :].bitcast(I32), in_=tab_scales[:, 4 * q : 4 * q + 4, :].bitcast(I32))
-        for q in range(4):
-            nc.gpsimd.dma_start(out=w2_sc_raw[32 * q : 32 * q + 8, :].bitcast(I32), in_=w2_scales[:, 4 * q : 4 * q + 4, :].bitcast(I32))
         gain_sb = keep.tile([P, PACK], F32, name="gain_sb")
 
         nc.sync.dma_start(list1[:], offs)
         tab = [keep.tile([P, T], I32, name=f"tab{a}", align_bytes=64) for a in range(PASSES)]
         w2_raw = keep.tile([P, PASSES, H], I32, name="w2_raw", align_bytes=64)
+        w1_rows = w1.rearrange("(a p j) c -> a p j c", p=P, j=PACK)
+        w1_first = keep.tile([P, PACK, H], F32, name="w1_first")
+        nc.sync.dma_start(out=w1_first[:], in_=w1_rows[0])
         nc.sync.dma_start(out=tab[0][:], in_=tab_words[0].rearrange("p t i -> p (t i)").bitcast(I32))
         nc.sync.dma_start(out=w2_raw[:], in_=w2_words.rearrange("a p c i -> p a (c i)").bitcast(I32))
+        for q in range(4):
+            nc.sync.dma_start(out=w2_sc_raw[32 * q : 32 * q + 8, :].bitcast(I32), in_=w2_scales[:, 4 * q : 4 * q + 4, :].bitcast(I32))
         nc.sync.dma_start(out=tab[1][:], in_=tab_words[1].rearrange("p t i -> p (t i)").bitcast(I32))
-        w1_raw = []
-        for a in range(PASSES):
-            rows = w1[512 * a : 512 * (a + 1), :].rearrange("(p j) c -> p j c", j=PACK)
-            for g in range(2):
-                raw = ring.tile([P, PACK, H // 2], F32, name=f"w1_raw{a}{g}", tag="w_raw", bufs=4)
-                nc.sync.dma_start(out=raw[:], in_=rows[:, :, g * H // 2 : (g + 1) * H // 2])
-                w1_raw.append(raw)
-
+        w1_last = [keep.tile([P, PACK, H // 2], F32, name=f"w1_last{g}", tag=f"w1_last{g}") for g in range(2)]
+        for g in range(2):
+            nc.sync.dma_start(out=w1_last[g][:], in_=w1_rows[1][:, :, g * H // 2 : (g + 1) * H // 2])
         nc.sync.dma_start(list2[:], offs2)
         nc.sync.dma_start(out=gain_sb[:], in_=gain.rearrange("(p i) -> p i", i=PACK))
         rg_rows = rg.rearrange("(p i) j -> p i j", i=PACK)
@@ -75,10 +79,9 @@ def tile_list_encounter_cell_watch_kernel(
             rg_sb.append(keep.tile([P, S], F32, name=f"rg{i}", tag=f"rg{i}"))
             page.append(keep.tile([P, T2], F32, name=f"page{i}"))
             wgs_sb.append(keep.tile([P, S], F32, name=f"wgs{i}", tag=f"wgs{i}"))
-            for hf in range(S // HALF):
-                cols = slice(hf * HALF, (hf + 1) * HALF)
+            for cols in pieces(i):
                 nc.sync.dma_start(out=rg_sb[i][:, cols], in_=rg_rows[:, i, cols])
-                if hf == 0:
+                if cols.start == 0:
                     nc.sync.dma_start(out=page[i][:], in_=page_rows[:, i, :])
                 for q in (0, 2, 1, 3):
                     nc.sync.dma_start(out=wgs_sb[i][32 * q : 32 * (q + 1), cols], in_=wgs_rows[:, i, cols])
@@ -111,87 +114,103 @@ def tile_list_encounter_cell_watch_kernel(
         w2_sc = keep.tile([P, H], U8, name="w2_sc", align_bytes=64)
         for a in range(PASSES):
             nc.vector.tensor_copy(
-                w2_codes[:, a, :].rearrange("p (i m) -> p m i", i=PACK),
-                w2_raw[:, a, :].bitcast(U32).rearrange("p (m i) -> p m i", i=PACK),
+                w2_codes[:, a, :].rearrange("p (i g m) -> p g i m", i=PACK, m=4),
+                w2_raw[:, a, :].bitcast(U32).rearrange("p (g m i) -> p g i m", i=PACK, m=4),
             )
-        nc.vector.tensor_copy(w2_sc[:].rearrange("p (i m) -> p m i", i=PACK), w2_sc_raw[:].rearrange("p (m i) -> p m i", i=PACK))
-        gather_words(1)
+        nc.vector.tensor_copy(
+            w2_sc[:].rearrange("p (i g m) -> p g i m", i=PACK, m=16), w2_sc_raw[:].rearrange("p (g m i) -> p g i m", i=PACK, m=16)
+        )
+        w1_bf = [keep.tile([P, H * PACK], BF16, name=f"w1_bf{a}", tag=f"w1_bf{a}", align_bytes=64) for a in range(PASSES)]
+        w1_codes = [keep.tile([P, H], U32, name=f"w1_codes{a}", align_bytes=64) for a in range(PASSES)]
+        w1_sc = [keep.tile([P, H], U8, name=f"w1_sc{a}", align_bytes=64) for a in range(PASSES)]
+        dealt = [t[:].rearrange("p (i m j) -> p m i j", i=PACK, j=PACK) for t in w1_bf]
 
-        w1_codes, w1_sc = [], []
-        for a in range(PASSES):
-            grouped = keep.tile([P, H * PACK], BF16, name=f"w1_bf{a}", tag=f"w1_bf{a}", align_bytes=64)
-            for g in range(2):
-                nc.vector.tensor_copy(
-                    grouped[:].rearrange("p (i m j) -> p m i j", i=PACK, j=PACK)[:, g * P // 2 : (g + 1) * P // 2],
-                    w1_raw[2 * a + g][:].rearrange("p j (m i) -> p m i j", i=PACK),
-                )
-            w1_codes.append(keep.tile([P, H], U32, name=f"w1_codes{a}", align_bytes=64))
-            w1_sc.append(keep.tile([P, H], U8, name=f"w1_sc{a}", align_bytes=64))
-            for g in range(2):
-                cols = slice(g * H // 2, (g + 1) * H // 2)
+        def quantise_w1(a, pieces):
+            width = H // pieces
+            for g in range(pieces):
+                cols = slice(g * width, (g + 1) * width)
                 nc.vector.quantize_mx(
-                    out=w1_codes[a][:, cols].bitcast(FP8X4), scales=w1_sc[a][:, cols], in_=grouped[:, g * 2 * H : (g + 1) * 2 * H]
+                    out=w1_codes[a][:, cols].bitcast(FP8X4), scales=w1_sc[a][:, cols], in_=w1_bf[a][:, g * PACK * width : (g + 1) * PACK * width]
                 )
 
-        def first_product(acc, codes, scales, unit):
+        nc.scalar.copy(dealt[0], w1_first[:].rearrange("p j (m i) -> p m i j", i=PACK))
+        nc.scalar.copy(dealt[1][:, : P // 2], w1_last[0][:].rearrange("p j (m i) -> p m i j", i=PACK))
+        quantise_w1(0, 1)
+        gather_words(1)
+        nc.vector.tensor_copy(dealt[1][:, P // 2 :], w1_last[1][:].rearrange("p j (m i) -> p m i j", i=PACK))
+        quantise_w1(1, 2)
+        ident = keep.tile([P, P], F32, name="ident")
+        make_identity(nc, ident[:])
+
+        sines, tanhs = {}, {}
+
+        def sine_part(unit):
+            i, hf = divmod(unit, 2)
+            rows = slice(P * i, P * (i + 1))
+            b_t = banks[(unit - 1) % 4]
+            for g in range(HALF // P):
+                cols = slice(hf * HALF + g * P, hf * HALF + (g + 1) * P)
+                for a in range(PASSES):
+                    nc.tensor.matmul_mx(
+                        out=b_t[:, g * P : (g + 1) * P],
+                        lhsT=v_codes[a][:, cols].bitcast(FP8X4),
+                        lhsT_scale=v_sc[4 * a : P, cols],
+                        rhs=w2_codes[:, a, rows].bitcast(FP8X4),
+                        rhs_scale=w2_sc[4 * a : P, rows],
+                        start=(a == 0),
+                        stop=(a == PASSES - 1),
+                    )
+            if unit == 0:
+                whole_biased = keep.tile([P, HALF], U32, name="whole_biased0", tag="w1_last0")[:]
+                turns = keep.tile([P, HALF], F32, name="turns0", tag="w1_last1")[:]
+            else:
+                whole_biased = ring.tile([P, HALF], U32, name="whole_biased")[:]
+                turns = ring.tile([P, HALF], F32, name="turns")[:]
+            nc.scalar.activation(whole_biased, b_t[:], ACT.Copy, bias=ROUNDER, scale=1.0 / TWO_PI)
+            nc.scalar.activation(turns, b_t[:], ACT.Copy, bias=0.0, scale=1.0 / TWO_PI)
+            minus_whole = ring.tile([P, HALF], F32, name="minus_whole")
+            nc.scalar.activation(minus_whole[:], whole_biased, ACT.Copy, bias=ROUNDER, scale=-1.0)
+            part = banks[4 + unit % 2]
+            for g in range(HALF // P):
+                block = slice(g * P, (g + 1) * P)
+                for n, term in enumerate((turns, minus_whole[:])):
+                    nc.tensor.matmul(part[:, block], term[:, block], ident[:], start=(n == 0), stop=(n == 1), is_transpose=True)
+            if hf == 0:
+                sines[i] = ring.tile([P, S], F32, name="sine")
+            nc.scalar.activation(sines[i][:, hf * HALF : (hf + 1) * HALF], part[:], ACT.Sin, scale=TWO_PI)
+
+        def tanh_part(unit):
             i, hf = divmod(unit, 2)
             rows = slice(P * i, P * (i + 1))
             cols = slice(hf * HALF, (hf + 1) * HALF)
+            acc = banks[unit % 4]
             for a in range(PASSES):
                 nc.tensor.matmul_mx(
                     out=acc[:],
-                    lhsT=codes(a)[:, rows].bitcast(FP8X4),
-                    lhsT_scale=scales(a)[:, rows],
+                    lhsT=w1_codes[a][:, rows].bitcast(FP8X4),
+                    lhsT_scale=w1_sc[a][:, rows],
                     rhs=v_codes[a][:, cols].bitcast(FP8X4),
                     rhs_scale=v_sc[4 * a : P, cols],
                     start=(a == 0),
                     stop=(a == PASSES - 1),
                 )
+            if hf == 0:
+                tanhs[i] = ring.tile([P, S], F32, name="tanh")
+            nc.scalar.activation(tanhs[i][:, cols], acc[:], ACT.Tanh)
 
-        sines, tanhs, hs = {}, {}, {}
-
-        def sine_part(unit):
-            b = psum.tile([P, HALF], F32, name="b", tag="bank_b")
-            first_product(b, lambda a: w2_codes[:, a, :], lambda a: w2_sc[4 * a : P, :], unit)
-            turns_biased = ring.tile([P, HALF], U32, name="turns_biased")
-            nc.scalar.activation(turns_biased[:], b[:], ACT.Copy, bias=ROUNDER, scale=1.0 / TWO_PI)
-            turns = ring.tile([P, HALF], F32, name="turns")
-            nc.scalar.activation(turns[:], turns_biased[:], ACT.Copy, bias=-ROUNDER, scale=1.0)
-            angle = ring.tile([P, HALF], F32, name="angle")
-            nc.vector.scalar_tensor_tensor(angle[:], turns[:], -TWO_PI, b[:], ALU.mult, ALU.add)
-            sines[unit] = ring.tile([P, HALF], F32, name="sine", bufs=4)
-            nc.scalar.activation(sines[unit][:], angle[:], ACT.Sin)
-
-        def tanh_part(unit):
-            acc = psum.tile([P, HALF], F32, name="acc", tag="bank_a")
-            first_product(acc, lambda a: w1_codes[a][:], lambda a: w1_sc[a][:], unit)
-            tanhs[unit] = ring.tile([P, HALF], F32, name="tanh", bufs=4)
-            nc.scalar.activation(tanhs[unit][:], acc[:], ACT.Tanh)
-
-        def ranged(unit):
-            i, hf = divmod(unit, 2)
-            tr = ring.tile([P, HALF], F32, name="tr")
-            nc.vector.tensor_tensor(tr[:], tanhs[unit][:], rg_sb[i][:, hf * HALF : (hf + 1) * HALF], ALU.mult)
-            return tr
-
-        def combine(unit, tr):
-            i = unit // 2
-            hs[unit] = ring.tile([P, HALF], F32, name="h")
-            nc.vector.scalar_tensor_tensor(hs[unit][:], sines[unit][:], gain_sb[:, i : i + 1], tr[:], ALU.mult, ALU.add)
-
-        def scatter(unit):
-            i, hf = divmod(unit, 2)
-            nc.vector.tensor_tensor(
-                page[i][:].indirect(list2[:, hf * HALF // 16 : (hf + 1) * HALF // 16]),
-                hs[unit][:],
-                wgs_sb[i][:, hf * HALF : (hf + 1) * HALF],
-                ALU.mult,
-            )
+        def update_page(i):
+            h = ring.tile([P, S], F32, name="h")
+            for cols in pieces(i):
+                nc.vector.tensor_tensor(h[:, cols], tanhs[i][:, cols], rg_sb[i][:, cols], ALU.mult)
+                nc.vector.scalar_tensor_tensor(h[:, cols], sines[i][:, cols], gain_sb[:, i : i + 1], h[:, cols], ALU.mult, ALU.add)
+                nc.vector.tensor_tensor(
+                    page[i][:].indirect(list2[:, cols.start // 16 : cols.stop // 16]), h[:, cols], wgs_sb[i][:, cols], ALU.mult
+                )
 
         w3_codes, w3_sc = [], []
 
         def quantise_w3(g):
-            raw = ring.tile([P, PACK, W3_HALF], F32, name=f"w3_raw{g}", tag="w_raw", bufs=4)
+            raw = keep.tile([P, PACK, W3_HALF], F32, name=f"w3_raw{g}", tag=("rg1", "wgs1")[g])
             nc.sync.dma_start(out=raw[:], in_=w3.rearrange("(p j) n -> p j n", j=PACK)[:, :, g * W3_HALF : (g + 1) * W3_HALF])
             grouped = keep.tile([P, W3_HALF * PACK], BF16, name=f"w3_bf{g}", tag=f"w1_bf{g}", align_bytes=64)
             nc.scalar.copy(
@@ -202,19 +221,11 @@ def tile_list_encounter_cell_watch_kernel(
             w3_sc.append(keep.tile([P, W3_HALF], U8, name=f"w3_sc{g}", align_bytes=64))
             nc.vector.quantize_mx(out=w3_codes[g][:].bitcast(FP8X4), scales=w3_sc[g][:], in_=grouped[:])
 
-        sine_part(0)
-        sine_part(1)
         for i in range(PACK):
-            units = (2 * i, 2 * i + 1)
-            for u in units:
-                tanh_part(u)
-            trs = [ranged(u) for u in units]
-            for u, tr in zip(units, trs):
-                combine(u, tr)
-            for u in units:
-                if u + 2 < 2 * PACK:
-                    sine_part(u + 2)
-                scatter(u)
+            for unit in (2 * i, 2 * i + 1):
+                tanh_part(unit)
+                sine_part(unit)
+            update_page(i)
         for g in range(2):
             quantise_w3(g)
 
@@ -238,8 +249,9 @@ def tile_list_encounter_cell_watch_kernel(
 
         def second_products(c):
             for pair in range(N // (2 * P)):
-                y1 = psum.tile([P, 2, CHUNK], F32, name="y1", tag="bank_a")
-                y2 = psum.tile([P, 2, CHUNK], F32, name="y2", tag="bank_b")
+                turn = (c * (N // (2 * P)) + pair) % 4
+                y1 = banks[turn][:].rearrange("p (e m) -> p e m", e=2)
+                y2 = banks[4 + turn][:].rearrange("p (e m) -> p e m", e=2)
                 for e in range(2):
                     n0 = (2 * pair + e) * P
                     nc.tensor.matmul_mx(
@@ -263,9 +275,9 @@ def tile_list_encounter_cell_watch_kernel(
                         stop=True,
                     )
                 y2_sb = ring.tile([P, 2, CHUNK], F32, name="y2_sb")
-                nc.scalar.copy(y2_sb[:], y2[:])
-                low = ring.tile([P, 2, CHUNK], F32, name="low", bufs=4)
-                nc.vector.tensor_tensor(low[:], y1[:], y2_sb[:], ALU.min)
+                nc.scalar.copy(y2_sb[:], y2)
+                low = ring.tile([P, 2, CHUNK], F32, name="low", bufs=6)
+                nc.vector.tensor_tensor(low[:], y1, y2_sb[:], ALU.min)
                 rows = out[2 * pair * P : 2 * (pair + 1) * P, c * CHUNK : (c + 1) * CHUNK]
                 nc.sync.dma_start(out=rows.rearrange("(e p) m -> p e m", p=P), in_=low[:])
 

@@ -49,38 +49,44 @@ def tile_list_encounter_cell_watch_kernel(
         tab_sc = keep.tile([P, T], U8, name="tab_sc", tag="v_codes1", align_bytes=64)
         w2_sc_raw = keep.tile([P, H], U8, name="w2_sc_raw", align_bytes=64)
         w4_sc = keep.tile([P, N], U8, name="w4_sc", align_bytes=64)
-        for plane in (w2_sc_raw, tab_sc, w4_sc):
+        nc.gpsimd.memset(tab_sc[:, : T // 2].bitcast(I32), 0)
+        nc.vector.memset(tab_sc[:, T // 2 :].bitcast(I32), 0)
+        for plane in (w2_sc_raw, w4_sc):
             nc.vector.memset(plane[:].bitcast(I32), 0)
-        for q in range(4):
-            nc.gpsimd.dma_start(out=tab_sc[32 * q : 32 * q + 8, :].bitcast(I32), in_=tab_scales[:, 4 * q : 4 * q + 4, :].bitcast(I32))
         gain_sb = keep.tile([P, PACK], F32, name="gain_sb")
 
         nc.sync.dma_start(list1[:], offs)
-        tab = [keep.tile([P, T], I32, name=f"tab{a}", align_bytes=64) for a in range(PASSES)]
+        tab = [keep.tile([P, T], I32, name=f"tab{a}", tag=f"tab{a}", align_bytes=64) for a in range(PASSES)]
         w2_raw = keep.tile([P, PASSES, H], I32, name="w2_raw", align_bytes=64)
         w1_rows = w1.rearrange("(a p j) c -> a p j c", p=P, j=PACK)
-        w1_first = keep.tile([P, PACK, H], F32, name="w1_first")
-        nc.sync.dma_start(out=w1_first[:], in_=w1_rows[0])
         nc.sync.dma_start(out=tab[0][:], in_=tab_words[0].rearrange("p t i -> p (t i)").bitcast(I32))
+        for q in range(4):
+            nc.sync.dma_start(out=tab_sc[32 * q : 32 * q + 8, :].bitcast(I32), in_=tab_scales[:, 4 * q : 4 * q + 4, :].bitcast(I32))
         nc.sync.dma_start(out=w2_raw[:], in_=w2_words.rearrange("a p c i -> p a (c i)").bitcast(I32))
+        nc.sync.dma_start(out=tab[1][:], in_=tab_words[1].rearrange("p t i -> p (t i)").bitcast(I32))
         for q in range(4):
             nc.sync.dma_start(out=w2_sc_raw[32 * q : 32 * q + 8, :].bitcast(I32), in_=w2_scales[:, 4 * q : 4 * q + 4, :].bitcast(I32))
-        nc.sync.dma_start(out=tab[1][:], in_=tab_words[1].rearrange("p t i -> p (t i)").bitcast(I32))
-        w1_last = [keep.tile([P, PACK, H // 2], F32, name=f"w1_last{g}", tag=f"w1_last{g}") for g in range(2)]
-        for g in range(2):
-            nc.sync.dma_start(out=w1_last[g][:], in_=w1_rows[1][:, :, g * H // 2 : (g + 1) * H // 2])
+        w1_raw = [keep.tile([P, PACK, H], F32, name=f"w1_raw{a}") for a in range(PASSES)]
+        for a in range(PASSES):
+            nc.sync.dma_start(out=w1_raw[a][:], in_=w1_rows[a])
         nc.sync.dma_start(list2[:], offs2)
         nc.sync.dma_start(out=gain_sb[:], in_=gain.rearrange("(p i) -> p i", i=PACK))
         rg_rows = rg.rearrange("(p i) j -> p i j", i=PACK)
         page_rows = page0.rearrange("(p i) t -> p i t", i=PACK)
         wgs_rows = wgs.rearrange("(p i) j -> p i j", i=PACK)
-        rg_sb, page, wgs_sb = [], [], []
+        page, wgs_sb = [], []
+        rg_sb = [keep.tile([P, S], F32, name=f"rg{i}", tag=f"rg{i}") for i in range(PACK)]
+        w3_raw = keep.tile([P, PACK, N], F32, name="w3_raw")
         for i in range(PACK):
-            rg_sb.append(keep.tile([P, S], F32, name=f"rg{i}", tag=f"rg{i}"))
+            if i == PACK - 1:
+                nc.sync.dma_start(out=w3_raw[:], in_=w3.rearrange("(p j) n -> p j n", j=PACK))
             page.append(keep.tile([P, T2], F32, name=f"page{i}"))
             wgs_sb.append(keep.tile([P, S], F32, name=f"wgs{i}", tag=f"wgs{i}"))
             for cols in pieces(i):
-                nc.sync.dma_start(out=rg_sb[i][:, cols], in_=rg_rows[:, i, cols])
+                if i <= 1:
+                    nc.sync.dma_start(out=rg_sb[i][:, cols], in_=rg_rows[:, i, cols])
+                if 1 <= i < PACK - 1:
+                    nc.sync.dma_start(out=rg_sb[i + 1][:], in_=rg_rows[:, i + 1, :])
                 if cols.start == 0:
                     nc.sync.dma_start(out=page[i][:], in_=page_rows[:, i, :])
                 for q in (0, 2, 1, 3):
@@ -133,13 +139,11 @@ def tile_list_encounter_cell_watch_kernel(
                     out=w1_codes[a][:, cols].bitcast(FP8X4), scales=w1_sc[a][:, cols], in_=w1_bf[a][:, g * PACK * width : (g + 1) * PACK * width]
                 )
 
-        nc.scalar.copy(dealt[0], w1_first[:].rearrange("p j (m i) -> p m i j", i=PACK))
-        nc.scalar.copy(dealt[1][:, : P // 2], w1_last[0][:].rearrange("p j (m i) -> p m i j", i=PACK))
-        quantise_w1(0, 1)
         gather_words(1)
-        nc.vector.tensor_copy(dealt[1][:, P // 2 :], w1_last[1][:].rearrange("p j (m i) -> p m i j", i=PACK))
-        quantise_w1(1, 2)
-        ident = keep.tile([P, P], F32, name="ident")
+        for a in range(PASSES):
+            nc.vector.tensor_copy(dealt[a], w1_raw[a][:].rearrange("p j (m i) -> p m i j", i=PACK))
+            quantise_w1(a, a + 1)
+        ident = keep.tile([P, P], F32, name="ident", tag="ident", align_bytes=64)
         make_identity(nc, ident[:])
 
         sines, tanhs = {}, {}
@@ -147,7 +151,7 @@ def tile_list_encounter_cell_watch_kernel(
         def sine_part(unit):
             i, hf = divmod(unit, 2)
             rows = slice(P * i, P * (i + 1))
-            b_t = banks[(unit - 1) % 4]
+            b_t = banks[(unit - 2) % 4]
             for g in range(HALF // P):
                 cols = slice(hf * HALF + g * P, hf * HALF + (g + 1) * P)
                 for a in range(PASSES):
@@ -160,12 +164,8 @@ def tile_list_encounter_cell_watch_kernel(
                         start=(a == 0),
                         stop=(a == PASSES - 1),
                     )
-            if unit == 0:
-                whole_biased = keep.tile([P, HALF], U32, name="whole_biased0", tag="w1_last0")[:]
-                turns = keep.tile([P, HALF], F32, name="turns0", tag="w1_last1")[:]
-            else:
-                whole_biased = ring.tile([P, HALF], U32, name="whole_biased")[:]
-                turns = ring.tile([P, HALF], F32, name="turns")[:]
+            whole_biased = ring.tile([P, HALF], U32, name="whole_biased")[:]
+            turns = ring.tile([P, HALF], F32, name="turns")[:]
             nc.scalar.activation(whole_biased, b_t[:], ACT.Copy, bias=ROUNDER, scale=1.0 / TWO_PI)
             nc.scalar.activation(turns, b_t[:], ACT.Copy, bias=0.0, scale=1.0 / TWO_PI)
             minus_whole = ring.tile([P, HALF], F32, name="minus_whole")
@@ -198,36 +198,50 @@ def tile_list_encounter_cell_watch_kernel(
                 tanhs[i] = ring.tile([P, S], F32, name="tanh")
             nc.scalar.activation(tanhs[i][:, cols], acc[:], ACT.Tanh)
 
-        def update_page(i):
-            h = ring.tile([P, S], F32, name="h")
-            for cols in pieces(i):
-                nc.vector.tensor_tensor(h[:, cols], tanhs[i][:, cols], rg_sb[i][:, cols], ALU.mult)
-                nc.vector.scalar_tensor_tensor(h[:, cols], sines[i][:, cols], gain_sb[:, i : i + 1], h[:, cols], ALU.mult, ALU.add)
-                nc.vector.tensor_tensor(
-                    page[i][:].indirect(list2[:, cols.start // 16 : cols.stop // 16]), h[:, cols], wgs_sb[i][:, cols], ALU.mult
-                )
+        hs = {}
 
-        w3_codes, w3_sc = [], []
+        def times_range(i, cols):
+            if cols.start == 0:
+                hs[i] = ring.tile([P, S], F32, name="h")
+            nc.vector.tensor_tensor(hs[i][:, cols], tanhs[i][:, cols], rg_sb[i][:, cols], ALU.mult)
 
-        def quantise_w3(g):
-            raw = keep.tile([P, PACK, W3_HALF], F32, name=f"w3_raw{g}", tag=("rg1", "wgs1")[g])
-            nc.sync.dma_start(out=raw[:], in_=w3.rearrange("(p j) n -> p j n", j=PACK)[:, :, g * W3_HALF : (g + 1) * W3_HALF])
-            grouped = keep.tile([P, W3_HALF * PACK], BF16, name=f"w3_bf{g}", tag=f"w1_bf{g}", align_bytes=64)
-            nc.scalar.copy(
-                grouped[:].rearrange("p (c e j) -> p c j e", e=4, j=PACK),
-                raw[:].rearrange("p j (c e) -> p c j e", e=4),
+        def add_sine(i, cols):
+            h = hs[i]
+            nc.vector.scalar_tensor_tensor(h[:, cols], sines[i][:, cols], gain_sb[:, i : i + 1], h[:, cols], ALU.mult, ALU.add)
+
+        def put(i, cols):
+            nc.vector.tensor_tensor(
+                page[i][:].indirect(list2[:, cols.start // 16 : cols.stop // 16]), hs[i][:, cols], wgs_sb[i][:, cols], ALU.mult
             )
-            w3_codes.append(keep.tile([P, W3_HALF], U32, name=f"w3_codes{g}", align_bytes=64))
-            w3_sc.append(keep.tile([P, W3_HALF], U8, name=f"w3_sc{g}", align_bytes=64))
-            nc.vector.quantize_mx(out=w3_codes[g][:].bitcast(FP8X4), scales=w3_sc[g][:], in_=grouped[:])
 
-        for i in range(PACK):
+        def features(i):
             for unit in (2 * i, 2 * i + 1):
                 tanh_part(unit)
+            for unit in (2 * i, 2 * i + 1):
                 sine_part(unit)
-            update_page(i)
+
+        whole = slice(0, S)
+        features(0)
+        for cols in pieces(0):
+            times_range(0, cols)
+            add_sine(0, cols)
+            put(0, cols)
+        features(1)
+        times_range(1, whole)
+        for i in range(1, PACK):
+            add_sine(i, whole)
+            if i + 1 < PACK:
+                features(i + 1)
+                times_range(i + 1, whole)
+            put(i, whole)
+        w3_bf = keep.tile([P, N * PACK], BF16, name="w3_bf", tag="ident", align_bytes=64)
+        w3_codes = keep.tile([P, N], U32, name="w3_codes", align_bytes=64)
+        w3_sc = [keep.tile([P, W3_HALF], U8, name=f"w3_sc{g}", align_bytes=64) for g in range(2)]
         for g in range(2):
-            quantise_w3(g)
+            cols = slice(g * W3_HALF, (g + 1) * W3_HALF)
+            grouped = w3_bf[:, g * W3_HALF * PACK : (g + 1) * W3_HALF * PACK]
+            nc.scalar.copy(grouped.rearrange("p (c e j) -> p c j e", e=4, j=PACK), w3_raw[:, :, cols].rearrange("p j (c e) -> p c j e", e=4))
+            nc.vector.quantize_mx(out=w3_codes[:, cols].bitcast(FP8X4), scales=w3_sc[g][:], in_=grouped)
 
         x_codes, x_sc = {}, {}
 
@@ -267,7 +281,7 @@ def tile_list_encounter_cell_watch_kernel(
                     g, n0 = divmod((2 * pair + e) * P, W3_HALF)
                     nc.tensor.matmul_mx(
                         out=y1[:, e, :],
-                        lhsT=w3_codes[g][:, n0 : n0 + P].bitcast(FP8X4),
+                        lhsT=w3_codes[:, g * W3_HALF + n0 : g * W3_HALF + n0 + P].bitcast(FP8X4),
                         lhsT_scale=w3_sc[g][:, n0 : n0 + P],
                         rhs=x_codes[c][:].bitcast(FP8X4),
                         rhs_scale=x_sc[c][:],

@@ -49,10 +49,11 @@ def tile_list_encounter_cell_watch_kernel(
         tab_sc = keep.tile([P, T], U8, name="tab_sc", tag="v_codes1", align_bytes=64)
         w2_sc_raw = keep.tile([P, H], U8, name="w2_sc_raw", align_bytes=64)
         w4_sc = keep.tile([P, N], U8, name="w4_sc", align_bytes=64)
-        nc.gpsimd.memset(tab_sc[:, : T // 2].bitcast(I32), 0)
-        nc.vector.memset(tab_sc[:, T // 2 :].bitcast(I32), 0)
-        for plane in (w2_sc_raw, w4_sc):
+        nc.gpsimd.memset(w2_sc_raw[:].bitcast(I32), 0)
+        for plane in (tab_sc, w4_sc):
             nc.vector.memset(plane[:].bitcast(I32), 0)
+        for q in range(4):
+            nc.gpsimd.dma_start(out=tab_sc[32 * q : 32 * q + 8, :].bitcast(I32), in_=tab_scales[:, 4 * q : 4 * q + 4, :].bitcast(I32))
         gain_sb = keep.tile([P, PACK], F32, name="gain_sb")
 
         nc.sync.dma_start(list1[:], offs)
@@ -60,12 +61,10 @@ def tile_list_encounter_cell_watch_kernel(
         w2_raw = keep.tile([P, PASSES, H], I32, name="w2_raw", align_bytes=64)
         w1_rows = w1.rearrange("(a p j) c -> a p j c", p=P, j=PACK)
         nc.sync.dma_start(out=tab[0][:], in_=tab_words[0].rearrange("p t i -> p (t i)").bitcast(I32))
-        for q in range(4):
-            nc.sync.dma_start(out=tab_sc[32 * q : 32 * q + 8, :].bitcast(I32), in_=tab_scales[:, 4 * q : 4 * q + 4, :].bitcast(I32))
         nc.sync.dma_start(out=w2_raw[:], in_=w2_words.rearrange("a p c i -> p a (c i)").bitcast(I32))
-        nc.sync.dma_start(out=tab[1][:], in_=tab_words[1].rearrange("p t i -> p (t i)").bitcast(I32))
         for q in range(4):
             nc.sync.dma_start(out=w2_sc_raw[32 * q : 32 * q + 8, :].bitcast(I32), in_=w2_scales[:, 4 * q : 4 * q + 4, :].bitcast(I32))
+        nc.sync.dma_start(out=tab[1][:], in_=tab_words[1].rearrange("p t i -> p (t i)").bitcast(I32))
         w1_raw = [keep.tile([P, PACK, H], F32, name=f"w1_raw{a}") for a in range(PASSES)]
         for a in range(PASSES):
             nc.sync.dma_start(out=w1_raw[a][:], in_=w1_rows[a])
@@ -105,7 +104,7 @@ def tile_list_encounter_cell_watch_kernel(
         for q in range(4):
             nc.sync.dma_start(out=w4_sc[32 * q : 32 * q + 4, :].bitcast(I32), in_=w4_scales[0, 4 * q : 4 * q + 4, :].bitcast(I32))
         v_codes = [keep.tile([P, S], U32, name=f"v_codes{a}", tag=f"v_codes{a}", align_bytes=64) for a in range(PASSES)]
-        v_sc = keep.tile([P, S], U8, name="v_sc", align_bytes=64)
+        v_sc = keep.tile([P, S], U8, name="v_sc", tag="tab0", align_bytes=64)
 
         def gather_words(a):
             for hf in range(S // HALF):
@@ -114,8 +113,8 @@ def tile_list_encounter_cell_watch_kernel(
                     tab[a][:].bitcast(U32).indirect(list1[:, hf * HALF // 16 : (hf + 1) * HALF // 16]),
                 )
 
-        nc.vector.tensor_copy(v_sc[:], tab_sc[:].indirect(list1[:]))
         gather_words(0)
+        nc.vector.tensor_copy(v_sc[:], tab_sc[:].indirect(list1[:]))
         w2_codes = keep.tile([P, PASSES, H], U32, name="w2_codes", align_bytes=64)
         w2_sc = keep.tile([P, H], U8, name="w2_sc", align_bytes=64)
         for a in range(PASSES):

import math
from contextlib import ExitStack

import concourse.mybir as mybir
from concourse.masks import make_identity

K, H, N, T, S, T2, M = 1024, 512, 768, 4096, 1024, 2048, 1024
FLOPS = 2 * (2 * K * H * S + 2 * H * N * M)

F32 = mybir.dt.float32
BF16 = mybir.dt.bfloat16
I32 = mybir.dt.int32
U32 = mybir.dt.uint32
U16 = mybir.dt.uint16
U8 = mybir.dt.uint8
FP8X4 = mybir.dt.float8_e4m3fn_x4
FP4X4 = mybir.dt.float4_e2m1fn_x4
ALU = mybir.AluOpType
ACT = mybir.ActivationFunctionType

P = 128
PACK = 4
PASSES = K // (P * PACK)
HALF = 512
CHUNK = 256
W3_HALF = N // 2
ROUNDER = 1.5 * 2.0**23
TWO_PI = 2.0 * math.pi


def pieces(i):
    return [slice(0, HALF), slice(HALF, S)] if i == 0 else [slice(0, S)]


def tile_list_encounter_cell_watch_kernel(
    tc, tab_words, tab_scales, offs, offs2, offs3, w1, w2_words, w2_scales, rg, gain, wgs, page0, wgt, w3, w4_words, w4_scales, out
):
    nc = tc.nc
    with ExitStack() as ctx:
        keep = ctx.enter_context(tc.tile_pool(name="keep", bufs=1))
        ring = ctx.enter_context(tc.tile_pool(name="ring", bufs=2))
        psum = ctx.enter_context(tc.psum_pool(name="psum", bufs=1))
        banks = [psum.tile([P, HALF], F32, name=f"bank{n}") for n in range(8)]

        list1 = keep.tile([P, S // 16], U16, name="list1")
        list2 = keep.tile([P, S // 16], U16, name="list2")
        list3 = keep.tile([P, M // 16], U16, name="list3")

        tab_sc = keep.tile([P, T], U8, name="tab_sc", tag="v_codes1", align_bytes=64)
        w2_sc_raw = keep.tile([P, H], U8, name="w2_sc_raw", align_bytes=64)
        w4_sc = keep.tile([P, N], U8, name="w4_sc", align_bytes=64)
        nc.gpsimd.memset(w2_sc_raw[:].bitcast(I32), 0)
        for plane in (tab_sc, w4_sc):
            nc.vector.memset(plane[:].bitcast(I32), 0)
        for q in range(4):
            nc.gpsimd.dma_start(out=tab_sc[32 * q : 32 * q + 8, :].bitcast(I32), in_=tab_scales[:, 4 * q : 4 * q + 4, :].bitcast(I32))
        gain_sb = keep.tile([P, PACK], F32, name="gain_sb")

        nc.sync.dma_start(list1[:], offs)
        tab = [keep.tile([P, T], I32, name=f"tab{a}", tag=f"tab{a}", align_bytes=64) for a in range(PASSES)]
        w2_raw = keep.tile([P, PASSES, H], I32, name="w2_raw", align_bytes=64)
        w1_rows = w1.rearrange("(a p j) c -> a p j c", p=P, j=PACK)
        nc.sync.dma_start(out=tab[0][:], in_=tab_words[0].rearrange("p t i -> p (t i)").bitcast(I32))
        nc.sync.dma_start(out=w2_raw[:], in_=w2_words.rearrange("a p c i -> p a (c i)").bitcast(I32))
        for q in range(4):
            nc.sync.dma_start(out=w2_sc_raw[32 * q : 32 * q + 8, :].bitcast(I32), in_=w2_scales[:, 4 * q : 4 * q + 4, :].bitcast(I32))
        nc.sync.dma_start(out=tab[1][:], in_=tab_words[1].rearrange("p t i -> p (t i)").bitcast(I32))
        w1_raw = [keep.tile([P, PACK, H], F32, name=f"w1_raw{a}") for a in range(PASSES)]
        for a in range(PASSES):
            nc.sync.dma_start(out=w1_raw[a][:], in_=w1_rows[a])
        nc.sync.dma_start(list2[:], offs2)
        nc.sync.dma_start(out=gain_sb[:], in_=gain.rearrange("(p i) -> p i", i=PACK))
        rg_rows = rg.rearrange("(p i) j -> p i j", i=PACK)
        page_rows = page0.rearrange("(p i) t -> p i t", i=PACK)
        wgs_rows = wgs.rearrange("(p i) j -> p i j", i=PACK)
        page, wgs_sb = [], []
        rg_sb = [keep.tile([P, S], F32, name=f"rg{i}", tag=f"rg{i}") for i in range(PACK)]
        w3_raw = keep.tile([P, PACK, N], F32, name="w3_raw")
        for i in range(PACK):
            if i == PACK - 1:
                nc.sync.dma_start(out=w3_raw[:], in_=w3.rearrange("(p j) n -> p j n", j=PACK))
            page.append(keep.tile([P, T2], F32, name=f"page{i}"))
            wgs_sb.append(keep.tile([P, S], F32, name=f"wgs{i}", tag=f"wgs{i}"))
            for cols in pieces(i):
                if i <= 1:
                    nc.sync.dma_start(out=rg_sb[i][:, cols], in_=rg_rows[:, i, cols])
                if 1 <= i < PACK - 1:
                    nc.sync.dma_start(out=rg_sb[i + 1][:], in_=rg_rows[:, i + 1, :])
                if cols.start == 0:
                    nc.sync.dma_start(out=page[i][:], in_=page_rows[:, i, :])
                for q in (0, 2, 1, 3):
                    nc.sync.dma_start(out=wgs_sb[i][32 * q : 32 * (q + 1), cols], in_=wgs_rows[:, i, cols])

        nc.sync.dma_start(list3[:], offs3)
        wgt_sb = keep.tile([P, M], F32, name="wgt_sb")
        nc.sync.dma_start(out=wgt_sb[:], in_=wgt)
        w4_codes = keep.tile([P, 2 * N], U8, name="w4_codes", align_bytes=64)
        nc.sync.dma_start(out=w4_codes[:].bitcast(I32), in_=w4_words[0].bitcast(I32))

        zero = keep.tile([P, 1], F32, name="zero")
        nc.vector.memset(zero[:], 0.0)
        warm = keep.tile([P, 1], F32, name="warm")
        nc.scalar.activation(warm[:], zero[:], ACT.Silu)
        for q in range(4):
            nc.sync.dma_start(out=w4_sc[32 * q : 32 * q + 4, :].bitcast(I32), in_=w4_scales[0, 4 * q : 4 * q + 4, :].bitcast(I32))
        v_codes = [keep.tile([P, S], U32, name=f"v_codes{a}", tag=f"v_codes{a}", align_bytes=64) for a in range(PASSES)]
        v_sc = keep.tile([P, S], U8, name="v_sc", tag="tab0", align_bytes=64)

        def gather_words(a):
            for hf in range(S // HALF):
                nc.vector.tensor_copy(
                    v_codes[a][:, hf * HALF : (hf + 1) * HALF],
                    tab[a][:].bitcast(U32).indirect(list1[:, hf * HALF // 16 : (hf + 1) * HALF // 16]),
                )

        gather_words(0)
        nc.vector.tensor_copy(v_sc[:], tab_sc[:].indirect(list1[:]))
        w2_codes = keep.tile([P, PASSES, H], U32, name="w2_codes", align_bytes=64)
        w2_sc = keep.tile([P, H], U8, name="w2_sc", align_bytes=64)
        for a in range(PASSES):
            nc.vector.tensor_copy(
                w2_codes[:, a, :].rearrange("p (i g m) -> p g i m", i=PACK, m=4),
                w2_raw[:, a, :].bitcast(U32).rearrange("p (g m i) -> p g i m", i=PACK, m=4),
            )
        nc.vector.tensor_copy(
            w2_sc[:].rearrange("p (i g m) -> p g i m", i=PACK, m=16), w2_sc_raw[:].rearrange("p (g m i) -> p g i m", i=PACK, m=16)
        )
        w1_bf = [keep.tile([P, H * PACK], BF16, name=f"w1_bf{a}", tag=f"w1_bf{a}", align_bytes=64) for a in range(PASSES)]
        w1_codes = [keep.tile([P, H], U32, name=f"w1_codes{a}", align_bytes=64) for a in range(PASSES)]
        w1_sc = [keep.tile([P, H], U8, name=f"w1_sc{a}", align_bytes=64) for a in range(PASSES)]
        dealt = [t[:].rearrange("p (i m j) -> p m i j", i=PACK, j=PACK) for t in w1_bf]

        def quantise_w1(a, pieces):
            width = H // pieces
            for g in range(pieces):
                cols = slice(g * width, (g + 1) * width)
                nc.vector.quantize_mx(
                    out=w1_codes[a][:, cols].bitcast(FP8X4), scales=w1_sc[a][:, cols], in_=w1_bf[a][:, g * PACK * width : (g + 1) * PACK * width]
                )

        gather_words(1)
        for a in range(PASSES):
            nc.vector.tensor_copy(dealt[a], w1_raw[a][:].rearrange("p j (m i) -> p m i j", i=PACK))
            quantise_w1(a, a + 1)
        ident = keep.tile([P, P], F32, name="ident", tag="ident", align_bytes=64)
        make_identity(nc, ident[:])

        sines, tanhs = {}, {}

        def sine_part(unit):
            i, hf = divmod(unit, 2)
            rows = slice(P * i, P * (i + 1))
            b_t = banks[(unit - 2) % 4]
            for g in range(HALF // P):
                cols = slice(hf * HALF + g * P, hf * HALF + (g + 1) * P)
                for a in range(PASSES):
                    nc.tensor.matmul_mx(
                        out=b_t[:, g * P : (g + 1) * P],
                        lhsT=v_codes[a][:, cols].bitcast(FP8X4),
                        lhsT_scale=v_sc[4 * a : P, cols],
                        rhs=w2_codes[:, a, rows].bitcast(FP8X4),
                        rhs_scale=w2_sc[4 * a : P, rows],
                        start=(a == 0),
                        stop=(a == PASSES - 1),
                    )
            whole_biased = ring.tile([P, HALF], U32, name="whole_biased")[:]
            turns = ring.tile([P, HALF], F32, name="turns")[:]
            nc.scalar.activation(whole_biased, b_t[:], ACT.Copy, bias=ROUNDER, scale=1.0 / TWO_PI)
            nc.scalar.activation(turns, b_t[:], ACT.Copy, bias=0.0, scale=1.0 / TWO_PI)
            minus_whole = ring.tile([P, HALF], F32, name="minus_whole")
            nc.scalar.activation(minus_whole[:], whole_biased, ACT.Copy, bias=ROUNDER, scale=-1.0)
            part = banks[4 + unit % 2]
            for g in range(HALF // P):
                block = slice(g * P, (g + 1) * P)
                for n, term in enumerate((turns, minus_whole[:])):
                    nc.tensor.matmul(part[:, block], term[:, block], ident[:], start=(n == 0), stop=(n == 1), is_transpose=True)
            if hf == 0:
                sines[i] = ring.tile([P, S], F32, name="sine")
            nc.scalar.activation(sines[i][:, hf * HALF : (hf + 1) * HALF], part[:], ACT.Sin, scale=TWO_PI)

        def tanh_part(unit):
            i, hf = divmod(unit, 2)
            rows = slice(P * i, P * (i + 1))
            cols = slice(hf * HALF, (hf + 1) * HALF)
            acc = banks[unit % 4]
            for a in range(PASSES):
                nc.tensor.matmul_mx(
                    out=acc[:],
                    lhsT=w1_codes[a][:, rows].bitcast(FP8X4),
                    lhsT_scale=w1_sc[a][:, rows],
                    rhs=v_codes[a][:, cols].bitcast(FP8X4),
                    rhs_scale=v_sc[4 * a : P, cols],
                    start=(a == 0),
                    stop=(a == PASSES - 1),
                )
            if hf == 0:
                tanhs[i] = ring.tile([P, S], F32, name="tanh")
            nc.scalar.activation(tanhs[i][:, cols], acc[:], ACT.Tanh)

        hs = {}

        def times_range(i, cols):
            if cols.start == 0:
                hs[i] = ring.tile([P, S], F32, name="h")
            nc.vector.tensor_tensor(hs[i][:, cols], tanhs[i][:, cols], rg_sb[i][:, cols], ALU.mult)

        def add_sine(i, cols):
            h = hs[i]
            nc.vector.scalar_tensor_tensor(h[:, cols], sines[i][:, cols], gain_sb[:, i : i + 1], h[:, cols], ALU.mult, ALU.add)

        def put(i, cols):
            nc.vector.tensor_tensor(
                page[i][:].indirect(list2[:, cols.start // 16 : cols.stop // 16]), hs[i][:, cols], wgs_sb[i][:, cols], ALU.mult
            )

        def features(i):
            for unit in (2 * i, 2 * i + 1):
                tanh_part(unit)
            for unit in (2 * i, 2 * i + 1):
                sine_part(unit)

        whole = slice(0, S)
        features(0)
        for cols in pieces(0):
            times_range(0, cols)
            add_sine(0, cols)
            put(0, cols)
        features(1)
        times_range(1, whole)
        for i in range(1, PACK):
            add_sine(i, whole)
            if i + 1 < PACK:
                features(i + 1)
                times_range(i + 1, whole)
            put(i, whole)
        w3_bf = keep.tile([P, N * PACK], BF16, name="w3_bf", tag="ident", align_bytes=64)
        w3_codes = keep.tile([P, N], U32, name="w3_codes", align_bytes=64)
        w3_sc = [keep.tile([P, W3_HALF], U8, name=f"w3_sc{g}", align_bytes=64) for g in range(2)]
        for g in range(2):
            cols = slice(g * W3_HALF, (g + 1) * W3_HALF)
            grouped = w3_bf[:, g * W3_HALF * PACK : (g + 1) * W3_HALF * PACK]
            nc.scalar.copy(grouped.rearrange("p (c e j) -> p c j e", e=4, j=PACK), w3_raw[:, :, cols].rearrange("p j (c e) -> p c j e", e=4))
            nc.vector.quantize_mx(out=w3_codes[:, cols].bitcast(FP8X4), scales=w3_sc[g][:], in_=grouped)

        x_codes, x_sc = {}, {}

        def gather_x(c):
            cols = slice(c * CHUNK, (c + 1) * CHUNK)
            xg = keep.tile([P, PACK, CHUNK], F32, name=f"xg{c}", tag=("wgs3", "rg3")[c % 2])
            for i in range(PACK):
                nc.vector.tensor_tensor(
                    xg[:, i, :], page[i][:].indirect(list3[:, c * CHUNK // 16 : (c + 1) * CHUNK // 16]), wgt_sb[:, cols], ALU.mult
                )
            xb = ring.tile([P, CHUNK * PACK], BF16, name="xb", align_bytes=64)
            nc.scalar.copy(xb[:].rearrange("p (c e i) -> p c i e", e=4, i=PACK), xg[:].rearrange("p i (c e) -> p c i e", e=4))
            return xb

        def quantise_x(c, xb):
            x_codes[c] = ring.tile([P, CHUNK], U32, name="x_codes", align_bytes=64)
            x_sc[c] = ring.tile([P, CHUNK], U8, name="x_sc", align_bytes=64)
            nc.vector.quantize_mx(out=x_codes[c][:].bitcast(FP8X4), scales=x_sc[c][:], in_=xb[:])

        def second_products(c):
            for pair in range(N // (2 * P)):
                turn = (c * (N // (2 * P)) + pair) % 4
                y1 = banks[turn][:].rearrange("p (e m) -> p e m", e=2)
                y2 = banks[4 + turn][:].rearrange("p (e m) -> p e m", e=2)
                for e in range(2):
                    n0 = (2 * pair + e) * P
                    nc.tensor.matmul_mx(
                        out=y2[:, e, :],
                        lhsT=w4_codes[:, 2 * n0 : 2 * (n0 + P)].bitcast(FP4X4),
                        lhsT_scale=w4_sc[:, n0 : n0 + P],
                        rhs=x_codes[c][:].bitcast(FP8X4),
                        rhs_scale=x_sc[c][:],
                        start=True,
                        stop=True,
                    )
                for e in range(2):
                    g, n0 = divmod((2 * pair + e) * P, W3_HALF)
                    nc.tensor.matmul_mx(
                        out=y1[:, e, :],
                        lhsT=w3_codes[:, g * W3_HALF + n0 : g * W3_HALF + n0 + P].bitcast(FP8X4),
                        lhsT_scale=w3_sc[g][:, n0 : n0 + P],
                        rhs=x_codes[c][:].bitcast(FP8X4),
                        rhs_scale=x_sc[c][:],
                        start=True,
                        stop=True,
                    )
                y2_sb = ring.tile([P, 2, CHUNK], F32, name="y2_sb")
                nc.scalar.copy(y2_sb[:], y2)
                low = ring.tile([P, 2, CHUNK], F32, name="low", bufs=6)
                nc.vector.tensor_tensor(low[:], y1, y2_sb[:], ALU.min)
                rows = out[2 * pair * P : 2 * (pair + 1) * P, c * CHUNK : (c + 1) * CHUNK]
                nc.sync.dma_start(out=rows.rearrange("(e p) m -> p e m", p=P), in_=low[:])

        chunks = M // CHUNK
        xbs = {0: gather_x(0)}
        for c in range(chunks):
            if c + 1 < chunks:
                xbs[c + 1] = gather_x(c + 1)
            quantise_x(c, xbs[c])
            if c >= 1:
                second_products(c - 1)
        second_products(chunks - 1)
